import numpy as np
CORES = [2,10,18,26,34,42,50,58,66,74,82,90,98,106,114,122,130,138,146,154,162,170,178,186,194,202,210,218,226,234,242,250,258,266,274,282,290,298,306,314,322,330,338,346,354,362,370,378,386,394,402,410,418,426,434,442,450,458,466,474,482,490,498,506]
N = 64
ROUNDS, B = 6, 32
GROUPS = [[h * 16 + (g + 3 * h) % 16 for h in range(4)] for g in range(16)]
def setup_inputs(rng):
    return {"x": rng.standard_normal((N, ROUNDS, 128, 4 * B), dtype=np.float32)}
def reference(x):
    y = np.empty_like(x)
    for g in GROUPS:
        for i, r in enumerate(g):
            for j, s in enumerate(g):
                y[r][:, :, j * B:(j + 1) * B] = x[s][:, :, i * B:(i + 1) * B]
    return {"y": y}

import concourse.bass as bass

SHIFT_03 = 0
SHIFT_12 = 12

SCRATCH = {
    "slot": ("dram", [4, 128, 32], "float32"),
}
SEMAPHORES = ["dg", "ic", "sent", "ld", "st", "own"]

LO, HI = 0x0F, 0xF0
E = 4


def rank_program(g, core, T, topo):
    rank = T.rank_of(core)
    if rank is None:
        return
    groups, B = T.tables["GROUPS"], T.tables["B"]
    rounds = T.x.shape[0]

    def member(c, i):
        r = T.rank_of(c)
        for grp in groups:
            if r in grp:
                return T.cores[grp[i]]

    def diag(c):
        return member(c, (topo.host(c) + 2) % 4)

    def rho(c):
        h = topo.host(c)
        shift = (SHIFT_03, SHIFT_12, -SHIFT_12, -SHIFT_03)[h]
        return (3 - h) * 128 + ((topo.chip(c) + shift) % 16) * 8 + core % 8

    h = topo.host(core)
    p, q, d = h ^ 1, 3 - h, (h + 2) % 4
    INR, CRS, RHO = member(core, p), member(core, q), rho(core)
    W = diag(RHO)

    n = {"ld": 0, "st": 0, "sent": 0, "dg": 0, "ic": 0}

    def load(pairs):
        for s, k, j in pairs:
            g.dma_start(T.slot[s], T.x[k, :, j * B:(j + 1) * B]).then_inc(T.sem.ld, 16)
            n["ld"] += 16
        g.wait_ge(T.sem.ld, n["ld"])

    def store(pairs):
        for s, k, j in pairs:
            g.dma_start(T.y[k, :, j * B:(j + 1) * B], T.slot[s]).then_inc(T.sem.st, 16)
            n["st"] += 16
        g.wait_ge(T.sem.st, n["st"])

    def send(sem, writes):
        trs = []
        for mask, (s, dst, s2) in zip((LO, HI), writes):
            rid, pid = topo.addr(dst, core)
            trs.append(bass.RemoteDMATransfer(dst_ids=[bass.DstId(rid=rid, pnc=pid)], dma_engine_mask=mask,
                                              remote_sem=sem, src=T.slot[s], dst=T.slot[s2]))
            n["sent"] += E
        g.remote_dma_fused(trs, local_sem=T.sem.sent)

    def arrived(name, writes):
        n[name] += E * writes
        g.wait_ge(T.sem.dg if name == "dg" else T.sem.ic, n[name])

    g.dma_start(T.y[:, :, h * B:(h + 1) * B], T.x[:, :, h * B:(h + 1) * B]).then_inc(T.sem.own, 16)

    if h % 2 == 0:
        load([(0, 0, d)])
        send(T.sem.dg, [(0, RHO, 0)])
        for k in range(rounds):
            a, b = k % 2, (k + 1) % 2
            arrived("ic", 2)
            store([(2, k, p), (3, k, q)])
            load([(2, k, p), (3, k, q)])
            send(T.sem.ic, [(2, INR, 2), (3, CRS, 3)])
            arrived("dg", 2)
            store([(b, k, d)])
            if k + 1 < rounds:
                load([(b, k + 1, d)])
                send(T.sem.dg, [(b, RHO, b), (a, W, a)])
            else:
                send(T.sem.dg, [(a, W, a)])
    else:
        load([(2, 0, p), (3, 0, q), (1, 0, d)])
        send(T.sem.ic, [(2, INR, 2), (3, CRS, 3)])
        for k in range(rounds):
            a, b = k % 2, (k + 1) % 2
            if k == 0:
                arrived("dg", 1)
            else:
                arrived("dg", 2)
                store([(b, k - 1, d)])
                load([(b, k, d)])
            send(T.sem.dg, [(b, RHO, a), (a, W, b)])
            arrived("ic", 2)
            store([(2, k, p), (3, k, q)])
            if k + 1 < rounds:
                load([(2, k + 1, p), (3, k + 1, q)])
                send(T.sem.ic, [(2, INR, 2), (3, CRS, 3)])
        arrived("dg", 1)
        store([((rounds - 1) % 2, rounds - 1, d)])

    g.wait_ge(T.sem.sent, n["sent"])
    g.wait_ge(T.sem.own, 16)
